import numpy as np
import ml_dtypes

BF16 = ml_dtypes.bfloat16


def bf(x):
    return np.asarray(x, np.float32).astype(BF16)


def f32(x):
    return np.asarray(x, np.float32)


def f64(x):
    return np.asarray(x).astype(np.float64)


def striped(idx):
    return np.concatenate([l.reshape(-1, 16).T for l in idx])


def rows(idx, k):
    return np.tile(np.repeat(idx, 16, axis=0), (k // (16 * 8), 1))


def look(tab, idx):
    return np.take_along_axis(f64(tab), rows(idx, len(tab)), axis=1)


K, S, V, N, M = 128, 2048, 1024, 1024, 256


def setup_inputs():
    return {"tab": f32(np.random.standard_normal((K, S))), "w": bf(np.random.standard_normal((K, M)) / np.sqrt(K)), "offs": striped(np.random.randint(0, S, (8, N)))}


def reference(tab, w, offs):
    idx = np.stack([g.T.reshape(-1) for g in np.split(offs, 8)])
    t = look(tab, idx)
    x = 0.75 * t + 0.25
    y = f64(w).T @ x
    return y

@@ -1,0 +1,47 @@
+import concourse.mybir as mybir
+
+F32 = mybir.dt.float32
+BF16 = mybir.dt.bfloat16
+U16 = mybir.dt.uint16
+MULT = mybir.AluOpType.mult
+ADD = mybir.AluOpType.add
+
+R, S = 128, 2048
+N, M = 1024, 256
+P = 128
+PIECE = 512
+COLS = PIECE // 16
+
+FLOPS = 2 * R * M * N
+
+
+def tile_lookup_deq_aff_none_kernel(tc, tab, w, offs, out):
+    nc = tc.nc
+    with (
+        tc.tile_pool(name="held", bufs=1) as held,
+        tc.psum_pool(name="psum", bufs=1) as psum,
+    ):
+        lists = held.tile([P, N // 16], U16, name="lists")
+        nc.sync.dma_start(lists[:], offs)
+        window = held.tile([R, S], F32, name="window")
+        nc.sync.dma_start(window[:], tab)
+        weights = held.tile([R, M], BF16, name="weights")
+        nc.scalar.dma_start(weights[:], w)
+
+        xs = []
+        for p in range(N // PIECE):
+            x = held.tile([R, PIECE], BF16, name=f"x{p}")
+            picked = window[:].indirect(lists[:, p * COLS : (p + 1) * COLS])
+            nc.vector.tensor_scalar(x[:], picked, 0.75, 0.25, MULT, ADD)
+            xs.append(x)
+
+        for p, x in enumerate(xs):
+            for b in range(M // P):
+                bank = psum.tile([P, PIECE], F32, name=f"bank{p}{b}")
+                nc.tensor.matmul(bank[:], weights[:, b * P : (b + 1) * P], x[:])
+                y = held.tile([P, PIECE], F32, name=f"y{p}{b}")
+                if p == N // PIECE - 1 and b == 0:
+                    nc.vector.tensor_copy(y[:], bank[:])
+                else:
+                    nc.scalar.copy(y[:], bank[:])
+                nc.sync.dma_start(out[b * P : (b + 1) * P, p * PIECE : (p + 1) * PIECE], y[:])

@@ -22,11 +22,11 @@ def tile_lookup_deq_aff_none_kernel(tc, tab, w, offs, out):
         tc.psum_pool(name="psum", bufs=1) as psum,
     ):
         lists = held.tile([P, N // 16], U16, name="lists")
-        nc.sync.dma_start(lists[:], offs)
         window = held.tile([R, S], F32, name="window")
-        nc.sync.dma_start(window[:], tab)
         weights = held.tile([R, M], BF16, name="weights")
-        nc.scalar.dma_start(weights[:], w)
+        nc.sync.dma_start(lists[:], offs)
+        nc.scalar.dma_start(window[:], tab)
+        nc.sync.dma_start(weights[:], w)
 
         xs = []
         for p in range(N // PIECE):
@@ -35,13 +35,21 @@ def tile_lookup_deq_aff_none_kernel(tc, tab, w, offs, out):
             nc.vector.tensor_scalar(x[:], picked, 0.75, 0.25, MULT, ADD)
             xs.append(x)
 
-        for p, x in enumerate(xs):
-            for b in range(M // P):
-                bank = psum.tile([P, PIECE], F32, name=f"bank{p}{b}")
-                nc.tensor.matmul(bank[:], weights[:, b * P : (b + 1) * P], x[:])
-                y = held.tile([P, PIECE], F32, name=f"y{p}{b}")
-                if p == N // PIECE - 1 and b == 0:
-                    nc.vector.tensor_copy(y[:], bank[:])
-                else:
-                    nc.scalar.copy(y[:], bank[:])
-                nc.sync.dma_start(out[b * P : (b + 1) * P, p * PIECE : (p + 1) * PIECE], y[:])
+        y0 = held.tile([P, M // P, PIECE], F32, name="y0")
+        for b in range(M // P):
+            bank = psum.tile([P, PIECE], F32, name=f"bank0{b}")
+            nc.tensor.matmul(bank[:], weights[:, b * P : (b + 1) * P], xs[0][:])
+            nc.scalar.copy(y0[:, b, :], bank[:])
+        nc.sync.dma_start(out[:, 0:PIECE].rearrange("(b p) j -> p b j", p=P), y0[:])
+
+        banks = []
+        for b in range(M // P):
+            bank = psum.tile([P, PIECE], F32, name=f"bank1{b}")
+            nc.tensor.matmul(bank[:], weights[:, b * P : (b + 1) * P], xs[1][:])
+            banks.append(bank)
+        y10 = held.tile([P, PIECE], F32, name="y10")
+        nc.vector.tensor_copy(y10[:], banks[0][:])
+        nc.sync.dma_start(out[0:P, PIECE:N], y10[:])
+        y11 = held.tile([P, PIECE], F32, name="y11")
+        nc.scalar.copy(y11[:], banks[1][:])
+        nc.scalar.dma_start(out[P:M, PIECE:N], y11[:])

@@ -10,6 +10,8 @@ R, S = 128, 2048
 N, M = 1024, 256
 P = 128
 PIECE = 512
+HALF = PIECE // 2
+WARM_UP = 12
 COLS = PIECE // 16
 
 FLOPS = 2 * R * M * N
@@ -26,7 +28,13 @@ def tile_lookup_deq_aff_none_kernel(tc, tab, w, offs, out):
         weights = held.tile([R, M], BF16, name="weights")
         nc.sync.dma_start(lists[:], offs)
         nc.scalar.dma_start(window[:], tab)
-        nc.sync.dma_start(weights[:], w)
+        nc.scalar.dma_start(weights[:], w)
+
+        zeros = held.tile([P, PIECE], BF16, name="zeros")
+        nc.vector.memset(zeros[:], 0.0)
+        idle = psum.tile([P, PIECE], F32, name="idle")
+        for i in range(WARM_UP):
+            nc.tensor.matmul(idle[:], zeros[:, 0:P], zeros[:])
 
         xs = []
         for p in range(N // PIECE):
@@ -35,21 +43,22 @@ def tile_lookup_deq_aff_none_kernel(tc, tab, w, offs, out):
             nc.vector.tensor_scalar(x[:], picked, 0.75, 0.25, MULT, ADD)
             xs.append(x)
 
-        y0 = held.tile([P, M // P, PIECE], F32, name="y0")
         for b in range(M // P):
             bank = psum.tile([P, PIECE], F32, name=f"bank0{b}")
             nc.tensor.matmul(bank[:], weights[:, b * P : (b + 1) * P], xs[0][:])
-            nc.scalar.copy(y0[:, b, :], bank[:])
-        nc.sync.dma_start(out[:, 0:PIECE].rearrange("(b p) j -> p b j", p=P), y0[:])
+            y0 = held.tile([P, PIECE], F32, name=f"y0{b}")
+            nc.scalar.copy(y0[:], bank[:])
+            nc.scalar.dma_start(out[b * P : (b + 1) * P, 0:PIECE], y0[:])
 
-        banks = []
-        for b in range(M // P):
-            bank = psum.tile([P, PIECE], F32, name=f"bank1{b}")
-            nc.tensor.matmul(bank[:], weights[:, b * P : (b + 1) * P], xs[1][:])
-            banks.append(bank)
-        y10 = held.tile([P, PIECE], F32, name="y10")
-        nc.vector.tensor_copy(y10[:], banks[0][:])
-        nc.sync.dma_start(out[0:P, PIECE:N], y10[:])
-        y11 = held.tile([P, PIECE], F32, name="y11")
-        nc.scalar.copy(y11[:], banks[1][:])
-        nc.scalar.dma_start(out[P:M, PIECE:N], y11[:])
+        y1 = [held.tile([P, PIECE], F32, name=f"y1{b}") for b in range(M // P)]
+        for h in range(2):
+            cols = slice(h * HALF, (h + 1) * HALF)
+            for b in range(M // P):
+                half = psum.tile([P, HALF], F32, name=f"half{h}{b}")
+                nc.tensor.matmul(half[:], weights[:, b * P : (b + 1) * P], xs[1][:, cols])
+                if b == 0:
+                    nc.vector.tensor_copy(y1[b][:, cols], half[:])
+                else:
+                    nc.scalar.copy(y1[b][:, cols], half[:])
+        nc.sync.dma_start(out[0:P, PIECE:N], y1[0][:])
+        nc.scalar.dma_start(out[P:M, PIECE:N], y1[1][:])

@@ -27,7 +27,8 @@ def tile_lookup_deq_aff_none_kernel(tc, tab, w, offs, out):
         window = held.tile([R, S], F32, name="window")
         weights = held.tile([R, M], BF16, name="weights")
         nc.sync.dma_start(lists[:], offs)
-        nc.scalar.dma_start(window[:], tab)
+        for queue, cols in ((nc.sync, slice(0, S // 2)), (nc.scalar, slice(S // 2, S))):
+            queue.dma_start(window[:, cols], tab[:, cols])
         nc.scalar.dma_start(weights[:], w)
 
         zeros = held.tile([P, PIECE], BF16, name="zeros")

import concourse.mybir as mybir

F32 = mybir.dt.float32
BF16 = mybir.dt.bfloat16
U16 = mybir.dt.uint16
MULT = mybir.AluOpType.mult
ADD = mybir.AluOpType.add

R, S = 128, 2048
N, M = 1024, 256
P = 128
PIECE = 512
HALF = PIECE // 2
WARM_UP = 12
COLS = PIECE // 16

FLOPS = 2 * R * M * N


def tile_lookup_deq_aff_none_kernel(tc, tab, w, offs, out):
    nc = tc.nc
    with (
        tc.tile_pool(name="held", bufs=1) as held,
        tc.psum_pool(name="psum", bufs=1) as psum,
    ):
        lists = held.tile([P, N // 16], U16, name="lists")
        window = held.tile([R, S], F32, name="window")
        weights = held.tile([R, M], BF16, name="weights")
        nc.sync.dma_start(lists[:], offs)
        for queue, cols in ((nc.sync, slice(0, S // 2)), (nc.scalar, slice(S // 2, S))):
            queue.dma_start(window[:, cols], tab[:, cols])
        nc.scalar.dma_start(weights[:], w)

        zeros = held.tile([P, PIECE], BF16, name="zeros")
        nc.vector.memset(zeros[:], 0.0)
        idle = psum.tile([P, PIECE], F32, name="idle")
        for i in range(WARM_UP):
            nc.tensor.matmul(idle[:], zeros[:, 0:P], zeros[:])

        xs = []
        for p in range(N // PIECE):
            x = held.tile([R, PIECE], BF16, name=f"x{p}")
            picked = window[:].indirect(lists[:, p * COLS : (p + 1) * COLS])
            nc.vector.tensor_scalar(x[:], picked, 0.75, 0.25, MULT, ADD)
            xs.append(x)

        for b in range(M // P):
            bank = psum.tile([P, PIECE], F32, name=f"bank0{b}")
            nc.tensor.matmul(bank[:], weights[:, b * P : (b + 1) * P], xs[0][:])
            y0 = held.tile([P, PIECE], F32, name=f"y0{b}")
            nc.scalar.copy(y0[:], bank[:])
            nc.scalar.dma_start(out[b * P : (b + 1) * P, 0:PIECE], y0[:])

        y1 = [held.tile([P, PIECE], F32, name=f"y1{b}") for b in range(M // P)]
        for h in range(2):
            cols = slice(h * HALF, (h + 1) * HALF)
            for b in range(M // P):
                half = psum.tile([P, HALF], F32, name=f"half{h}{b}")
                nc.tensor.matmul(half[:], weights[:, b * P : (b + 1) * P], xs[1][:, cols])
                if b == 0:
                    nc.vector.tensor_copy(y1[b][:, cols], half[:])
                else:
                    nc.scalar.copy(y1[b][:, cols], half[:])
        nc.sync.dma_start(out[0:P, PIECE:N], y1[0][:])
        nc.scalar.dma_start(out[P:M, PIECE:N], y1[1][:])
